import numpy as np, ml_dtypes
CORES = [16,23,24,31,64,71]
N = 6
import mx_ref
NC, G = 256, 4
C = np.float32(0.043)
BF = ml_dtypes.bfloat16
def cut(t, i, w=512):
    return t[:, w * i:w * i + w]
def tile(rs):
    return np.stack(rs, axis=2).reshape(128, -1).astype(BF)
def layer(w, X):
    out = []
    for i in range(G):
        for t in range(len(X)):
            p = mx_ref.matmul(mx_ref.quantize(cut(w, len(X) * i + t)), X[t])
            z = p if t == 0 else z + p
        out.append(z)
    return out
def act(Z):
    return [np.maximum(z, 0) * C for z in Z]
def setup_inputs(rng):
    def f(*shape):
        return mx_ref.flush((rng.standard_normal(shape, dtype=np.float32) * np.exp2(rng.integers(-2, 3, shape[:-1] + (1,)))).astype(BF))
    return {"x": f(N, 128, 4 * NC), "w1": f(N, 128, G * 512), "w2": f(N, 128, 512)}
def setup_inputs_blocks(rng):
    d = setup_inputs(rng)
    for k in ("x", "w1", "w2"): d[k] = mx_ref.spread(d[k], rng, 2)
    return d
def setup_inputs_wide(rng):
    d = setup_inputs(rng)
    for k in ("x", "w1", "w2"): d[k] = mx_ref.flush((d[k].astype(np.float32) * np.exp2(rng.integers(-6, 7, (N, 1, 1))).astype(np.float32)).astype(BF))
    return d
def reference(x, w1, w2):
    X = [mx_ref.quantize(x[j]) for j in range(N)]
    y = np.zeros((N, 128, NC), np.float32)
    for c in range(N):
        for r in range(N):
            p = mx_ref.matmul(mx_ref.quantize(w2[r]), mx_ref.quantize(tile(act(layer(w1[r], [X[c]])))))
            y[c] = p if r == 0 else y[c] + p
    return {"y": y}

@@ -1,0 +1,275 @@
+import numpy as np
+from concourse.bass import DstId, RemoteDMATransfer
+from concourse.mybir import dt, AluOpType, ActivationFunctionType
+
+SIM = 80
+NC = 256
+W1C, W2C = 512, 128
+WC = W1C + W2C
+BANK = 512
+RING = 6
+OWN_BANK, FAR_BANK = 6, 7
+SCALE = float(np.float32(0.043))
+
+SCRATCH = {
+    "xb": ("sbuf", [128, 4 * NC], "bfloat16"),
+    "w1b": ("sbuf", [128, 4 * W1C], "bfloat16"),
+    "w2b": ("sbuf", [128, 4 * W2C], "bfloat16"),
+    "xc": ("sbuf", [128, NC], "float8_e4m3fn_x4"), "xs": ("sbuf", [128, NC], "uint8"),
+    "wc": ("sbuf", [128, WC], "float8_e4m3fn_x4"), "ws": ("sbuf", [128, WC], "uint8"),
+    "pc": ("sbuf", [128, WC], "float8_e4m3fn_x4"), "ps": ("sbuf", [128, WC], "uint8"),
+    "xc0": ("sbuf", [128, NC], "float8_e4m3fn_x4"), "xs0": ("sbuf", [128, NC], "uint8"),
+    "xc1": ("sbuf", [128, NC], "float8_e4m3fn_x4"), "xs1": ("sbuf", [128, NC], "uint8"),
+    "rc": ("sbuf", [128, NC], "float8_e4m3fn_x4"), "rs": ("sbuf", [128, NC], "uint8"),
+    "ry": ("sbuf", [128, NC], "float32"),
+    "yo0": ("sbuf", [128, NC], "float32"), "yo1": ("sbuf", [128, NC], "float32"),
+    "yl0": ("sbuf", [128, NC], "float32"), "yl1": ("sbuf", [128, NC], "float32"),
+    "yt": ("sbuf", [128, NC], "float32"), "yf": ("sbuf", [128, NC], "float32"),
+    "acc": ("psum", [128, 8 * BANK], "float32"),
+}
+for _i in range(6):
+    SCRATCH["h%d" % _i] = ("sbuf", [128, 4 * NC], "bfloat16")
+    SCRATCH["hc%d" % _i] = ("sbuf", [128, NC], "float8_e4m3fn_x4")
+    SCRATCH["hs%d" % _i] = ("sbuf", [128, NC], "uint8")
+SEMAPHORES = ["lx", "lw1", "lw2", "st0", "st1",
+              "te", "ve", "sc",
+              "x0", "x1", "wp", "y0", "y1",
+              "rxc", "rxs", "ryf",
+              "ls"]
+
+
+def engines(mask):
+    return [1 << e for e in range(mask.bit_length()) if mask >> e & 1]
+
+
+def make_plan(cores, topo):
+    need = lambda s, d: 0 if topo.may_write(s, d) else 1
+    peer, todo = {}, {}
+    for a in cores:
+        peer[a] = [b for b in cores if b != a and topo.chip(b) == topo.chip(a)][0]
+    for a in cores:
+        b = peer[a]
+        if a > b:
+            continue
+        far = [c for c in cores if c not in (a, b)]
+        best = None
+        for i in range(len(far)):
+            for j in range(i + 1, len(far)):
+                mine = [far[i], far[j]]
+                rest = [c for c in far if c not in mine]
+                cost = [need(c, w) + need(w, c) for w, cs in ((a, mine), (b, rest)) for c in cs]
+                key = (max(cost), sum(cost))
+                if best is None or key < best[0]:
+                    best = (key, mine, rest)
+        for w, cs in ((a, best[1]), (b, best[2])):
+            todo[w] = sorted(cs, key=lambda c: (need(c, w), cores.index(c)))
+    workers = {c: [w for w in cores if c in todo[w]] for c in cores}
+    back = {c: sorted(workers[c], key=lambda w: (need(c, w) + need(w, c), todo[w].index(c))) for c in cores}
+    helpers = lambda s, d: [h for h in range(SIM) if h not in cores and topo.chip(h) == topo.chip(s)
+                            and topo.die(h) == topo.die(s) and topo.may_write(h, d)]
+    via = {}
+    for s in cores:
+        far = [w for w in workers[s] if need(s, w)]
+        for k, w in enumerate(far):
+            hs = helpers(s, w)
+            via["x", s, w] = (hs[0], hs[1]) if len(far) == 1 else (hs[k], hs[k])
+        far = [c for c in todo[s] if need(s, c)]
+        for k, c in enumerate(far):
+            via["y", s, c] = helpers(s, c)[k]
+    return peer, todo, workers, back, via
+
+
+def rank_program(g, core, T, topo):
+    cores = list(T.cores)
+    peer, todo, workers, back, via = make_plan(cores, topo)
+    S = T.sem
+    sent = [0]
+
+    def away(c):
+        far = [d for d in cores if topo.chip(d) != topo.chip(c)][0]
+        return engines(topo.mask(c, far))
+
+    def codes(t):
+        return t[:].bitcast(dt.uint8)
+
+    def send(parts):
+        trs = []
+        for dst, es, sem, out, in_ in parts:
+            rid, pid, _ = topo.addr(dst)
+            trs.append(RemoteDMATransfer(dst_ids=[DstId(rid=rid, pnc=pid)], dma_engine_mask=sum(es), remote_sem=S[sem],
+                                         srcs=[in_], dsts=[out]))
+            sent[0] += len(es)
+        g.remote_dma_fused(trs, local_sem=S["ls"])
+
+    rank = T.rank_of(core)
+    if rank is None:
+        es = away(core)
+        for (kind, s, d), hs in sorted(via.items()):
+            if kind != "x" or core not in hs:
+                continue
+            k, n = todo[d].index(s), len(es) // 2
+            if core == hs[0]:
+                g.wait_ge(S["rxc"], n)
+                send([(d, es, "x%d" % k, codes(T["xc%d" % k]), codes(T["rc"]))])
+            if core == hs[1]:
+                g.wait_ge(S["rxs"], n)
+                send([(d, es, "x%d" % k, T["xs%d" % k][:], T["rs"][:])])
+        for (kind, s, d), h in sorted(via.items(), key=str):
+            if kind == "y" and core == h:
+                k = back[d].index(s)
+                g.wait_ge(S["ryf"], len(es))
+                send([(d, es, "y%d" % k, T["yl%d" % k][:], T["ry"][:])])
+        if sent[0]:
+            g.wait_ge(S["ls"], sent[0])
+        return
+
+    es = away(core)
+    half = len(es) // 2
+    inner = [e for e in engines(topo.mask(core, peer[core])) if e not in es]
+    Q = {"te": g.tensor, "ve": g.vector, "sc": g.scalar, "g": g, "sy": g.sync}
+    cnt = {"te": 0, "ve": 0, "sc": 0}
+    seen = {}
+
+    def wait(q, sem, val):
+        if seen.get((q, sem), 0) < val:
+            Q[q].wait_ge(S[sem], val)
+            seen[q, sem] = val
+
+    def done(q, ins):
+        ins.then_inc(S[q], 1)
+        cnt[q] += 1
+        return cnt[q]
+
+    g.sync.dma_start(T.xb[:], T.x[:]).then_inc(S["lx"], 16)
+    g.sync.dma_start(T.w1b[:], T.w1[:]).then_inc(S["lw1"], 16)
+    g.sync.dma_start(T.w2b[:], T.w2[:]).then_inc(S["lw2"], 16)
+    wait("ve", "lx", 16)
+    qx = done("ve", g.vector.quantize_mx(T.xc[:], T.xs[:], T.xb[:]))
+    wait("ve", "lw1", 16)
+    qw1 = done("ve", g.vector.quantize_mx(T.wc[:, 0:W1C], T.ws[:, 0:W1C], T.w1b[:]))
+    wait("ve", "lw2", 16)
+    qw2 = done("ve", g.vector.quantize_mx(T.wc[:, W1C:WC], T.ws[:, W1C:WC], T.w2b[:]))
+
+    wait("g", "ve", qx)
+    for part in (0, 1):
+        legs = []
+        for k, w in enumerate(workers[core]):
+            p = todo[w].index(core)
+            e = es[k * half:(k + 1) * half]
+            hs = via.get(("x", core, w))
+            if hs is None:
+                dst, sem, c, s = w, "x%d" % p, "xc%d" % p, "xs%d" % p
+            else:
+                dst, sem, c, s = hs[part], ("rxc", "rxs")[part], "rc", "rs"
+            legs.append((dst, e, sem, codes(T[c]), codes(T["xc"])) if part == 0 else (dst, e, sem, T[s][:], T["xs"][:]))
+        send(legs)
+    wait("g", "ve", qw2)
+    send([(peer[core], inner, "wp", codes(T["pc"]), codes(T["wc"]))])
+    send([(peer[core], inner, "wp", T["ps"][:], T["ws"][:])])
+
+    direct = [topo.may_write(c, core) for c in todo[core]]
+    pairs, placed = [(None, 0)], False
+    for k in (0, 1):
+        if not direct[k] and not placed:
+            pairs.append((None, 1))
+            placed = True
+        pairs += [(k, 0), (k, 1)]
+    if not placed:
+        pairs.append((None, 1))
+    arrive = [2 * half if d else 2 * len(es) for d in direct]
+    freed = {}
+    made = {}
+    copied = [0]
+    own_done = [0]
+
+    def first(i):
+        tile, w = pairs[i]
+        if tile is None:
+            wait("te", "ve", qx)
+            xc, xs = T.xc, T.xs
+        else:
+            wait("te", "x%d" % tile, arrive[tile])
+            xc, xs = T["xc%d" % tile], T["xs%d" % tile]
+        if w == 0:
+            wait("te", "ve", qw1)
+            wc, ws = T.wc, T.ws
+        else:
+            wait("te", "wp", 2 * len(inner))
+            wc, ws = T.pc, T.ps
+        h = T["h%d" % i]
+        last = {"sc": 0, "ve": 0}
+        for b in range(4):
+            k = 4 * i + b
+            bank = k % RING
+            if k >= RING:
+                wait("te", freed[k - RING][0], freed[k - RING][1])
+            z = T.acc[:, BANK * bank:BANK * bank + NC]
+            n = done("te", g.tensor.matmul_mx(z, wc[:, 128 * b:128 * b + 128], ws[:, 128 * b:128 * b + 128],
+                                              xc[:], xs[:], True, True))
+            out = h[:, b:4 * NC:4]
+            if b % 2 == 0:
+                wait("sc", "te", n)
+                last["sc"] = done("sc", g.scalar.activation(out, z, ActivationFunctionType.Relu, scale=SCALE))
+                freed[k] = ("sc", last["sc"])
+            else:
+                wait("ve", "te", n)
+                last["ve"] = done("ve", g.vector.tensor_scalar(out, z, 0.0, SCALE, AluOpType.max, AluOpType.mult))
+                freed[k] = ("ve", last["ve"])
+        wait("ve", "sc", last["sc"])
+        wait("ve", "ve", last["ve"])
+        made[i] = done("ve", g.vector.quantize_mx(T["hc%d" % i][:], T["hs%d" % i][:], h[:]))
+
+    def second(i):
+        tile, w = pairs[i]
+        wc, ws = (T.wc, T.ws) if w == 0 else (T.pc, T.ps)
+        bank = OWN_BANK if tile is None else FAR_BANK
+        if tile is not None and w == 0 and copied[0]:
+            wait("te", "sc", copied[0])
+        wait("te", "ve", max(made[i], qw2))
+        yp = T.acc[:, BANK * bank:BANK * bank + NC]
+        n = done("te", g.tensor.matmul_mx(yp, wc[:, W1C:WC], ws[:, W1C:WC], T["hc%d" % i][:], T["hs%d" % i][:],
+                                          w == 0, w == 1))
+        if tile is None:
+            own_done[0] = n
+        elif w == 1:
+            c = todo[core][tile]
+            yo = T["yo%d" % tile]
+            wait("sc", "te", n)
+            copied[0] = done("sc", g.scalar.activation(yo[:], yp, ActivationFunctionType.Copy))
+            wait("g", "sc", copied[0])
+            h = via.get(("y", core, c))
+            if h is None:
+                k = back[c].index(core)
+                send([(c, es, "y%d" % k, T["yl%d" % k][:], yo[:])])
+            else:
+                send([(h, es, "ryf", T["ry"][:], yo[:])])
+
+    pending = None
+    for i in range(6):
+        tile, w = pairs[i]
+        if pending is not None and tile is not None and w == 0 and pairs[i - 1][0] is None:
+            second(pending)
+            pending = None
+        first(i)
+        if pending is not None:
+            second(pending)
+        pending = i
+    second(pending)
+
+    mine = T.acc[:, BANK * OWN_BANK:BANK * OWN_BANK + NC]
+    came = [len(es), len(es)]
+    wait("ve", "te", own_done[0])
+    wait("ve", "y0", came[0])
+    t = done("ve", g.vector.tensor_tensor(T.yt[:], mine, T.yl0[:], AluOpType.add))
+    wait("ve", "ve", t)
+    wait("ve", "y1", came[1])
+    for k, q in ((0, "sy"), (1, "sc")):
+        a, b = k * NC // 2, (k + 1) * NC // 2
+        t = done("ve", g.vector.tensor_tensor(T.yf[:, a:b], T.yt[:, a:b], T.yl1[:, a:b], AluOpType.add))
+        wait(q, "ve", t)
+        Q[q].dma_start(T.y[:, a:b], T.yf[:, a:b]).then_inc(S["st%d" % k], 16)
+        wait(q, "st%d" % k, 16)
+    wait("g", "te", cnt["te"])
+    wait("g", "sc", cnt["sc"])
+    wait("g", "ls", sent[0])
+    wait("g", "ve", cnt["ve"])

@@ -4,12 +4,14 @@ from concourse.mybir import dt, AluOpType, ActivationFunctionType
 
 SIM = 80
 NC = 256
+HC = NC // 2
 W1C, W2C = 512, 128
 WC = W1C + W2C
 BANK = 512
 RING = 6
 OWN_BANK, FAR_BANK = 6, 7
 SCALE = float(np.float32(0.043))
+CUTS = (((0, NC),), ((0, HC), (HC, NC)))
 
 SCRATCH = {
     "xb": ("sbuf", [128, 4 * NC], "bfloat16"),
@@ -21,20 +23,20 @@ SCRATCH = {
     "xc0": ("sbuf", [128, NC], "float8_e4m3fn_x4"), "xs0": ("sbuf", [128, NC], "uint8"),
     "xc1": ("sbuf", [128, NC], "float8_e4m3fn_x4"), "xs1": ("sbuf", [128, NC], "uint8"),
     "rc": ("sbuf", [128, NC], "float8_e4m3fn_x4"), "rs": ("sbuf", [128, NC], "uint8"),
-    "ry": ("sbuf", [128, NC], "float32"),
+    "ry0": ("sbuf", [128, NC], "float32"), "ry1": ("sbuf", [128, NC], "float32"),
     "yo0": ("sbuf", [128, NC], "float32"), "yo1": ("sbuf", [128, NC], "float32"),
     "yl0": ("sbuf", [128, NC], "float32"), "yl1": ("sbuf", [128, NC], "float32"),
     "yt": ("sbuf", [128, NC], "float32"), "yf": ("sbuf", [128, NC], "float32"),
     "acc": ("psum", [128, 8 * BANK], "float32"),
 }
-for _i in range(6):
+for _i in range(8):
     SCRATCH["h%d" % _i] = ("sbuf", [128, 4 * NC], "bfloat16")
     SCRATCH["hc%d" % _i] = ("sbuf", [128, NC], "float8_e4m3fn_x4")
     SCRATCH["hs%d" % _i] = ("sbuf", [128, NC], "uint8")
 SEMAPHORES = ["lx", "lw1", "lw2", "st0", "st1",
               "te", "ve", "sc",
-              "x0", "x1", "wp", "y0", "y1",
-              "rxc", "rxs", "ryf",
+              "x0", "x1", "wp", "y0", "y1a", "y1b",
+              "rxc", "rxs", "ry0", "ry1",
               "ls"]
 
 
@@ -44,6 +46,7 @@ def engines(mask):
 
 def make_plan(cores, topo):
     need = lambda s, d: 0 if topo.may_write(s, d) else 1
+    detour = lambda c, w: need(c, w) + need(w, c)
     peer, todo = {}, {}
     for a in cores:
         peer[a] = [b for b in cores if b != a and topo.chip(b) == topo.chip(a)][0]
@@ -57,31 +60,49 @@ def make_plan(cores, topo):
             for j in range(i + 1, len(far)):
                 mine = [far[i], far[j]]
                 rest = [c for c in far if c not in mine]
-                cost = [need(c, w) + need(w, c) for w, cs in ((a, mine), (b, rest)) for c in cs]
+                cost = [detour(c, w) for w, cs in ((a, mine), (b, rest)) for c in cs]
                 key = (max(cost), sum(cost))
                 if best is None or key < best[0]:
                     best = (key, mine, rest)
         for w, cs in ((a, best[1]), (b, best[2])):
             todo[w] = sorted(cs, key=lambda c: (need(c, w), cores.index(c)))
     workers = {c: [w for w in cores if c in todo[w]] for c in cores}
-    back = {c: sorted(workers[c], key=lambda w: (need(c, w) + need(w, c), todo[w].index(c))) for c in cores}
-    helpers = lambda s, d: [h for h in range(SIM) if h not in cores and topo.chip(h) == topo.chip(s)
-                            and topo.die(h) == topo.die(s) and topo.may_write(h, d)]
-    via = {}
-    for s in cores:
-        far = [w for w in workers[s] if need(s, w)]
-        for k, w in enumerate(far):
-            hs = helpers(s, w)
-            via["x", s, w] = (hs[0], hs[1]) if len(far) == 1 else (hs[k], hs[k])
-        far = [c for c in todo[s] if need(s, c)]
-        for k, c in enumerate(far):
-            via["y", s, c] = helpers(s, c)[k]
-    return peer, todo, workers, back, via
+    back = {c: sorted(workers[c], key=lambda w: (detour(c, w), todo[w].index(c))) for c in cores}
+
+    def helpers(s, d):
+        return [h for h in range(SIM) if h not in cores and topo.chip(h) == topo.chip(s)
+                and topo.die(h) == topo.die(s) and topo.may_write(h, d)]
+
+    def x_calls(c):
+        calls = []
+        for urgent in (True, False):
+            group = [w for w in workers[c] if (detour(c, w) > 0) == urgent]
+            n = len(group)
+            if n == 0:
+                continue
+            cd, sc = [], []
+            for i, w in enumerate(group):
+                if need(c, w) == 0:
+                    stops = (w, w)
+                elif sum(need(c, v) for v in group) == 1:
+                    stops = helpers(c, w)[:2]
+                else:
+                    stops = (helpers(c, w)[i],) * 2
+                cd.append((stops[0], (i, n), w, True))
+                sc.append((stops[1], (i, n), w, False))
+            calls += [cd, sc]
+        return calls
+
+    def y_legs(w, k):
+        c = todo[w][k]
+        return [(c if need(w, c) == 0 else helpers(w, c)[j], c, a, b) for j, (a, b) in enumerate(CUTS[k])]
+
+    return peer, todo, back, x_calls, y_legs
 
 
 def rank_program(g, core, T, topo):
     cores = list(T.cores)
-    peer, todo, workers, back, via = make_plan(cores, topo)
+    peer, todo, back, x_calls, y_legs = make_plan(cores, topo)
     S = T.sem
     sent = [0]
 
@@ -89,42 +110,53 @@ def rank_program(g, core, T, topo):
         far = [d for d in cores if topo.chip(d) != topo.chip(c)][0]
         return engines(topo.mask(c, far))
 
-    def codes(t):
-        return t[:].bitcast(dt.uint8)
+    es = away(core)
+
+    def share(part):
+        i, n = part
+        return es[i * len(es) // n:(i + 1) * len(es) // n]
+
+    def codes(t, a, b):
+        return t[:, a:b].bitcast(dt.uint8)
 
     def send(parts):
         trs = []
-        for dst, es, sem, out, in_ in parts:
+        for dst, e, sem, out, in_ in parts:
             rid, pid, _ = topo.addr(dst)
-            trs.append(RemoteDMATransfer(dst_ids=[DstId(rid=rid, pnc=pid)], dma_engine_mask=sum(es), remote_sem=S[sem],
+            trs.append(RemoteDMATransfer(dst_ids=[DstId(rid=rid, pnc=pid)], dma_engine_mask=sum(e), remote_sem=S[sem],
                                          srcs=[in_], dsts=[out]))
-            sent[0] += len(es)
+            sent[0] += len(e)
         g.remote_dma_fused(trs, local_sem=S["ls"])
+
+    def y_slot(w, c, a):
+        if w == back[c][0]:
+            return "yl0", "y0"
+        return "yl1", "y1a" if a == 0 else "y1b"
 
     rank = T.rank_of(core)
     if rank is None:
-        es = away(core)
-        for (kind, s, d), hs in sorted(via.items()):
-            if kind != "x" or core not in hs:
-                continue
-            k, n = todo[d].index(s), len(es) // 2
-            if core == hs[0]:
-                g.wait_ge(S["rxc"], n)
-                send([(d, es, "x%d" % k, codes(T["xc%d" % k]), codes(T["rc"]))])
-            if core == hs[1]:
-                g.wait_ge(S["rxs"], n)
-                send([(d, es, "x%d" % k, T["xs%d" % k][:], T["rs"][:])])
-        for (kind, s, d), h in sorted(via.items(), key=str):
-            if kind == "y" and core == h:
-                k = back[d].index(s)
-                g.wait_ge(S["ryf"], len(es))
-                send([(d, es, "y%d" % k, T["yl%d" % k][:], T["ry"][:])])
+        for s in cores:
+            for call in x_calls(s):
+                for dst, part, w, is_codes in call:
+                    if dst != core:
+                        continue
+                    k = todo[w].index(s)
+                    g.wait_ge(S["rxc" if is_codes else "rxs"], len(share(part)))
+                    if is_codes:
+                        send([(w, es, "x%d" % k, codes(T["xc%d" % k], 0, NC), codes(T.rc, 0, NC))])
+                    else:
+                        send([(w, es, "x%d" % k, T["xs%d" % k][:], T.rs[:])])
+        for w in cores:
+            for k in (0, 1):
+                for dst, c, a, b in y_legs(w, k):
+                    if dst == core:
+                        g.wait_ge(S["ry%d" % k], len(es))
+                        buf, sem = y_slot(w, c, a)
+                        send([(c, es, sem, T[buf][:, a:b], T["ry%d" % k][:, a:b])])
         if sent[0]:
             g.wait_ge(S["ls"], sent[0])
         return
 
-    es = away(core)
-    half = len(es) // 2
     inner = [e for e in engines(topo.mask(core, peer[core])) if e not in es]
     Q = {"te": g.tensor, "ve": g.vector, "sc": g.scalar, "g": g, "sy": g.sync}
     cnt = {"te": 0, "ve": 0, "sc": 0}
@@ -151,39 +183,39 @@ def rank_program(g, core, T, topo):
     qw2 = done("ve", g.vector.quantize_mx(T.wc[:, W1C:WC], T.ws[:, W1C:WC], T.w2b[:]))
 
     wait("g", "ve", qx)
-    for part in (0, 1):
+    for call in x_calls(core):
         legs = []
-        for k, w in enumerate(workers[core]):
-            p = todo[w].index(core)
-            e = es[k * half:(k + 1) * half]
-            hs = via.get(("x", core, w))
-            if hs is None:
-                dst, sem, c, s = w, "x%d" % p, "xc%d" % p, "xs%d" % p
+        for dst, part, w, is_codes in call:
+            k = todo[w].index(core)
+            c, s, sc, ss = ("xc%d" % k, "xs%d" % k, "x%d" % k, "x%d" % k) if dst == w else ("rc", "rs", "rxc", "rxs")
+            if is_codes:
+                legs.append((dst, share(part), sc, codes(T[c], 0, NC), codes(T.xc, 0, NC)))
             else:
-                dst, sem, c, s = hs[part], ("rxc", "rxs")[part], "rc", "rs"
-            legs.append((dst, e, sem, codes(T[c]), codes(T["xc"])) if part == 0 else (dst, e, sem, T[s][:], T["xs"][:]))
+                legs.append((dst, share(part), ss, T[s][:], T.xs[:]))
         send(legs)
     wait("g", "ve", qw2)
-    send([(peer[core], inner, "wp", codes(T["pc"]), codes(T["wc"]))])
-    send([(peer[core], inner, "wp", T["ps"][:], T["ws"][:])])
+    send([(peer[core], inner, "wp", codes(T.pc, 0, WC), codes(T.wc, 0, WC))])
+    send([(peer[core], inner, "wp", T.ps[:], T.ws[:])])
 
-    direct = [topo.may_write(c, core) for c in todo[core]]
-    pairs, placed = [(None, 0)], False
+    arrive = [0, 0]
+    for k, c in enumerate(todo[core]):
+        for call in x_calls(c):
+            for dst, part, w, is_codes in call:
+                if w == core:
+                    arrive[k] += len(share(part)) if dst == w else len(es)
+    units = [(None, 0, 0, NC)]
     for k in (0, 1):
-        if not direct[k] and not placed:
-            pairs.append((None, 1))
-            placed = True
-        pairs += [(k, 0), (k, 1)]
-    if not placed:
-        pairs.append((None, 1))
-    arrive = [2 * half if d else 2 * len(es) for d in direct]
+        for a, b in CUTS[k]:
+            units += [(k, 0, a, b), (k, 1, a, b)]
+    units.append((None, 1, 0, NC))
     freed = {}
     made = {}
     copied = [0]
     own_done = [0]
 
     def first(i):
-        tile, w = pairs[i]
+        tile, w, ca, cb = units[i]
+        n = cb - ca
         if tile is None:
             wait("te", "ve", qx)
             xc, xs = T.xc, T.xs
@@ -203,72 +235,83 @@ def rank_program(g, core, T, topo):
             bank = k % RING
             if k >= RING:
                 wait("te", freed[k - RING][0], freed[k - RING][1])
-            z = T.acc[:, BANK * bank:BANK * bank + NC]
-            n = done("te", g.tensor.matmul_mx(z, wc[:, 128 * b:128 * b + 128], ws[:, 128 * b:128 * b + 128],
-                                              xc[:], xs[:], True, True))
-            out = h[:, b:4 * NC:4]
+            z = T.acc[:, BANK * bank:BANK * bank + n]
+            m = done("te", g.tensor.matmul_mx(z, wc[:, 128 * b:128 * b + 128], ws[:, 128 * b:128 * b + 128],
+                                              xc[:, ca:cb], xs[:, ca:cb], True, True))
+            out = h[:, b:4 * n:4]
             if b % 2 == 0:
-                wait("sc", "te", n)
+                wait("sc", "te", m)
                 last["sc"] = done("sc", g.scalar.activation(out, z, ActivationFunctionType.Relu, scale=SCALE))
                 freed[k] = ("sc", last["sc"])
             else:
-                wait("ve", "te", n)
+                wait("ve", "te", m)
                 last["ve"] = done("ve", g.vector.tensor_scalar(out, z, 0.0, SCALE, AluOpType.max, AluOpType.mult))
                 freed[k] = ("ve", last["ve"])
         wait("ve", "sc", last["sc"])
         wait("ve", "ve", last["ve"])
-        made[i] = done("ve", g.vector.quantize_mx(T["hc%d" % i][:], T["hs%d" % i][:], h[:]))
+        made[i] = done("ve", g.vector.quantize_mx(T["hc%d" % i][:, 0:n], T["hs%d" % i][:, 0:n], h[:, 0:4 * n]))
 
     def second(i):
-        tile, w = pairs[i]
+        tile, w, ca, cb = units[i]
+        n = cb - ca
         wc, ws = (T.wc, T.ws) if w == 0 else (T.pc, T.ps)
         bank = OWN_BANK if tile is None else FAR_BANK
         if tile is not None and w == 0 and copied[0]:
             wait("te", "sc", copied[0])
         wait("te", "ve", max(made[i], qw2))
-        yp = T.acc[:, BANK * bank:BANK * bank + NC]
-        n = done("te", g.tensor.matmul_mx(yp, wc[:, W1C:WC], ws[:, W1C:WC], T["hc%d" % i][:], T["hs%d" % i][:],
-                                          w == 0, w == 1))
+        yp = T.acc[:, BANK * bank:BANK * bank + n]
+        m = done("te", g.tensor.matmul_mx(yp, wc[:, W1C:WC], ws[:, W1C:WC],
+                                          T["hc%d" % i][:, 0:n], T["hs%d" % i][:, 0:n], w == 0, w == 1))
         if tile is None:
-            own_done[0] = n
+            own_done[0] = m
         elif w == 1:
-            c = todo[core][tile]
             yo = T["yo%d" % tile]
-            wait("sc", "te", n)
-            copied[0] = done("sc", g.scalar.activation(yo[:], yp, ActivationFunctionType.Copy))
+            wait("sc", "te", m)
+            copied[0] = done("sc", g.scalar.activation(yo[:, ca:cb], yp, ActivationFunctionType.Copy))
             wait("g", "sc", copied[0])
-            h = via.get(("y", core, c))
-            if h is None:
-                k = back[c].index(core)
-                send([(c, es, "y%d" % k, T["yl%d" % k][:], yo[:])])
-            else:
-                send([(h, es, "ryf", T["ry"][:], yo[:])])
+            for dst, c, a, b in y_legs(core, tile):
+                if a == ca:
+                    buf, sem = y_slot(core, c, a) if dst == c else ("ry%d" % tile, "ry%d" % tile)
+                    send([(dst, es, sem, T[buf][:, a:b], yo[:, a:b])])
+
+    early, late = back[core]
+    n0 = len(es) * len(y_legs(early, todo[early].index(core)))
+    n1 = len(y_legs(late, todo[late].index(core)))
+    own_last = not any(topo.may_write(c, core) for c in todo[core])
+    added = 0
 
     pending = None
-    for i in range(6):
-        tile, w = pairs[i]
-        if pending is not None and tile is not None and w == 0 and pairs[i - 1][0] is None:
+    for i in range(len(units)):
+        if pending is not None and (units[i][0] is None) != (units[pending][0] is None):
             second(pending)
             pending = None
+            if own_last and i == len(units) - 1:
+                wait("ve", "y0", n0)
+                for k in range(n1):
+                    wait("ve", ("y1a", "y1b")[k], len(es))
+                added = done("ve", g.vector.tensor_tensor(T.yt[:], T.yl0[:], T.yl1[:], AluOpType.add))
         first(i)
         if pending is not None:
             second(pending)
         pending = i
     second(pending)
 
-    mine = T.acc[:, BANK * OWN_BANK:BANK * OWN_BANK + NC]
-    came = [len(es), len(es)]
     wait("ve", "te", own_done[0])
-    wait("ve", "y0", came[0])
-    t = done("ve", g.vector.tensor_tensor(T.yt[:], mine, T.yl0[:], AluOpType.add))
-    wait("ve", "ve", t)
-    wait("ve", "y1", came[1])
+    base = BANK * OWN_BANK
+    if not own_last:
+        wait("ve", "y0", n0)
+        added = done("ve", g.vector.tensor_tensor(T.yt[:], T.acc[:, base:base + NC], T.yl0[:], AluOpType.add))
+    wait("ve", "ve", added)
     for k, q in ((0, "sy"), (1, "sc")):
-        a, b = k * NC // 2, (k + 1) * NC // 2
-        t = done("ve", g.vector.tensor_tensor(T.yf[:, a:b], T.yt[:, a:b], T.yl1[:, a:b], AluOpType.add))
+        a, b = k * HC, (k + 1) * HC
+        if k < n1:
+            wait("ve", ("y1a", "y1b")[k], len(es))
+        rest = T.acc[:, base + a:base + b] if own_last else T.yl1[:, a:b]
+        t = done("ve", g.vector.tensor_tensor(T.yf[:, a:b], rest, T.yt[:, a:b], AluOpType.add))
         wait(q, "ve", t)
         Q[q].dma_start(T.y[:, a:b], T.yf[:, a:b]).then_inc(S["st%d" % k], 16)
-        wait(q, "st%d" % k, 16)
+    wait("sy", "st0", 16)
+    wait("sc", "st1", 16)
     wait("g", "te", cnt["te"])
     wait("g", "sc", cnt["sc"])
     wait("g", "ls", sent[0])

import numpy as np
from concourse.bass import DstId, RemoteDMATransfer
from concourse.mybir import dt, AluOpType, ActivationFunctionType

SIM = 80
NC = 256
HC = NC // 2
W1C, W2C = 512, 128
WC = W1C + W2C
BANK = 512
RING = 6
OWN_BANK, FAR_BANK = 6, 7
SCALE = float(np.float32(0.043))
CUTS = (((0, NC),), ((0, HC), (HC, NC)))

SCRATCH = {
    "xb": ("sbuf", [128, 4 * NC], "bfloat16"),
    "w1b": ("sbuf", [128, 4 * W1C], "bfloat16"),
    "w2b": ("sbuf", [128, 4 * W2C], "bfloat16"),
    "xc": ("sbuf", [128, NC], "float8_e4m3fn_x4"), "xs": ("sbuf", [128, NC], "uint8"),
    "wc": ("sbuf", [128, WC], "float8_e4m3fn_x4"), "ws": ("sbuf", [128, WC], "uint8"),
    "pc": ("sbuf", [128, WC], "float8_e4m3fn_x4"), "ps": ("sbuf", [128, WC], "uint8"),
    "xc0": ("sbuf", [128, NC], "float8_e4m3fn_x4"), "xs0": ("sbuf", [128, NC], "uint8"),
    "xc1": ("sbuf", [128, NC], "float8_e4m3fn_x4"), "xs1": ("sbuf", [128, NC], "uint8"),
    "rc": ("sbuf", [128, NC], "float8_e4m3fn_x4"), "rs": ("sbuf", [128, NC], "uint8"),
    "ry0": ("sbuf", [128, NC], "float32"), "ry1": ("sbuf", [128, NC], "float32"),
    "yo0": ("sbuf", [128, NC], "float32"), "yo1": ("sbuf", [128, NC], "float32"),
    "yl0": ("sbuf", [128, NC], "float32"), "yl1": ("sbuf", [128, NC], "float32"),
    "yt": ("sbuf", [128, NC], "float32"), "yf": ("sbuf", [128, NC], "float32"),
    "acc": ("psum", [128, 8 * BANK], "float32"),
}
for _i in range(8):
    SCRATCH["h%d" % _i] = ("sbuf", [128, 4 * NC], "bfloat16")
    SCRATCH["hc%d" % _i] = ("sbuf", [128, NC], "float8_e4m3fn_x4")
    SCRATCH["hs%d" % _i] = ("sbuf", [128, NC], "uint8")
SEMAPHORES = ["lx", "lw1", "lw2", "st0", "st1",
              "te", "ve", "sc",
              "x0", "x1", "wp", "y0", "y1a", "y1b",
              "rxc", "rxs", "ry0", "ry1",
              "ls"]


def engines(mask):
    return [1 << e for e in range(mask.bit_length()) if mask >> e & 1]


def make_plan(cores, topo):
    need = lambda s, d: 0 if topo.may_write(s, d) else 1
    detour = lambda c, w: need(c, w) + need(w, c)
    peer, todo = {}, {}
    for a in cores:
        peer[a] = [b for b in cores if b != a and topo.chip(b) == topo.chip(a)][0]
    for a in cores:
        b = peer[a]
        if a > b:
            continue
        far = [c for c in cores if c not in (a, b)]
        best = None
        for i in range(len(far)):
            for j in range(i + 1, len(far)):
                mine = [far[i], far[j]]
                rest = [c for c in far if c not in mine]
                cost = [detour(c, w) for w, cs in ((a, mine), (b, rest)) for c in cs]
                key = (max(cost), sum(cost))
                if best is None or key < best[0]:
                    best = (key, mine, rest)
        for w, cs in ((a, best[1]), (b, best[2])):
            todo[w] = sorted(cs, key=lambda c: (need(c, w), cores.index(c)))
    workers = {c: [w for w in cores if c in todo[w]] for c in cores}
    back = {c: sorted(workers[c], key=lambda w: (detour(c, w), todo[w].index(c))) for c in cores}

    def helpers(s, d):
        return [h for h in range(SIM) if h not in cores and topo.chip(h) == topo.chip(s)
                and topo.die(h) == topo.die(s) and topo.may_write(h, d)]

    def x_calls(c):
        calls = []
        for urgent in (True, False):
            group = [w for w in workers[c] if (detour(c, w) > 0) == urgent]
            n = len(group)
            if n == 0:
                continue
            cd, sc = [], []
            for i, w in enumerate(group):
                if need(c, w) == 0:
                    stops = (w, w)
                elif sum(need(c, v) for v in group) == 1:
                    stops = helpers(c, w)[:2]
                else:
                    stops = (helpers(c, w)[i],) * 2
                cd.append((stops[0], (i, n), w, True))
                sc.append((stops[1], (i, n), w, False))
            calls += [cd, sc]
        return calls

    def y_legs(w, k):
        c = todo[w][k]
        return [(c if need(w, c) == 0 else helpers(w, c)[j], c, a, b) for j, (a, b) in enumerate(CUTS[k])]

    return peer, todo, back, x_calls, y_legs


def rank_program(g, core, T, topo):
    cores = list(T.cores)
    peer, todo, back, x_calls, y_legs = make_plan(cores, topo)
    S = T.sem
    sent = [0]

    def away(c):
        far = [d for d in cores if topo.chip(d) != topo.chip(c)][0]
        return engines(topo.mask(c, far))

    es = away(core)

    def share(part):
        i, n = part
        return es[i * len(es) // n:(i + 1) * len(es) // n]

    def codes(t, a, b):
        return t[:, a:b].bitcast(dt.uint8)

    def send(parts):
        trs = []
        for dst, e, sem, out, in_ in parts:
            rid, pid, _ = topo.addr(dst)
            trs.append(RemoteDMATransfer(dst_ids=[DstId(rid=rid, pnc=pid)], dma_engine_mask=sum(e), remote_sem=S[sem],
                                         srcs=[in_], dsts=[out]))
            sent[0] += len(e)
        g.remote_dma_fused(trs, local_sem=S["ls"])

    def y_slot(w, c, a):
        if w == back[c][0]:
            return "yl0", "y0"
        return "yl1", "y1a" if a == 0 else "y1b"

    rank = T.rank_of(core)
    if rank is None:
        for s in cores:
            for call in x_calls(s):
                for dst, part, w, is_codes in call:
                    if dst != core:
                        continue
                    k = todo[w].index(s)
                    g.wait_ge(S["rxc" if is_codes else "rxs"], len(share(part)))
                    if is_codes:
                        send([(w, es, "x%d" % k, codes(T["xc%d" % k], 0, NC), codes(T.rc, 0, NC))])
                    else:
                        send([(w, es, "x%d" % k, T["xs%d" % k][:], T.rs[:])])
        for w in cores:
            for k in (0, 1):
                for dst, c, a, b in y_legs(w, k):
                    if dst == core:
                        g.wait_ge(S["ry%d" % k], len(es))
                        buf, sem = y_slot(w, c, a)
                        send([(c, es, sem, T[buf][:, a:b], T["ry%d" % k][:, a:b])])
        if sent[0]:
            g.wait_ge(S["ls"], sent[0])
        return

    inner = [e for e in engines(topo.mask(core, peer[core])) if e not in es]
    Q = {"te": g.tensor, "ve": g.vector, "sc": g.scalar, "g": g, "sy": g.sync}
    cnt = {"te": 0, "ve": 0, "sc": 0}
    seen = {}

    def wait(q, sem, val):
        if seen.get((q, sem), 0) < val:
            Q[q].wait_ge(S[sem], val)
            seen[q, sem] = val

    def done(q, ins):
        ins.then_inc(S[q], 1)
        cnt[q] += 1
        return cnt[q]

    g.sync.dma_start(T.xb[:], T.x[:]).then_inc(S["lx"], 16)
    g.sync.dma_start(T.w1b[:], T.w1[:]).then_inc(S["lw1"], 16)
    g.sync.dma_start(T.w2b[:], T.w2[:]).then_inc(S["lw2"], 16)
    wait("ve", "lx", 16)
    qx = done("ve", g.vector.quantize_mx(T.xc[:], T.xs[:], T.xb[:]))
    wait("ve", "lw1", 16)
    qw1 = done("ve", g.vector.quantize_mx(T.wc[:, 0:W1C], T.ws[:, 0:W1C], T.w1b[:]))
    wait("ve", "lw2", 16)
    qw2 = done("ve", g.vector.quantize_mx(T.wc[:, W1C:WC], T.ws[:, W1C:WC], T.w2b[:]))

    wait("g", "ve", qx)
    for call in x_calls(core):
        legs = []
        for dst, part, w, is_codes in call:
            k = todo[w].index(core)
            c, s, sc, ss = ("xc%d" % k, "xs%d" % k, "x%d" % k, "x%d" % k) if dst == w else ("rc", "rs", "rxc", "rxs")
            if is_codes:
                legs.append((dst, share(part), sc, codes(T[c], 0, NC), codes(T.xc, 0, NC)))
            else:
                legs.append((dst, share(part), ss, T[s][:], T.xs[:]))
        send(legs)
    wait("g", "ve", qw2)
    send([(peer[core], inner, "wp", codes(T.pc, 0, WC), codes(T.wc, 0, WC))])
    send([(peer[core], inner, "wp", T.ps[:], T.ws[:])])

    arrive = [0, 0]
    for k, c in enumerate(todo[core]):
        for call in x_calls(c):
            for dst, part, w, is_codes in call:
                if w == core:
                    arrive[k] += len(share(part)) if dst == w else len(es)
    units = [(None, 0, 0, NC)]
    for k in (0, 1):
        for a, b in CUTS[k]:
            units += [(k, 0, a, b), (k, 1, a, b)]
    units.append((None, 1, 0, NC))
    freed = {}
    made = {}
    copied = [0]
    own_done = [0]

    def first(i):
        tile, w, ca, cb = units[i]
        n = cb - ca
        if tile is None:
            wait("te", "ve", qx)
            xc, xs = T.xc, T.xs
        else:
            wait("te", "x%d" % tile, arrive[tile])
            xc, xs = T["xc%d" % tile], T["xs%d" % tile]
        if w == 0:
            wait("te", "ve", qw1)
            wc, ws = T.wc, T.ws
        else:
            wait("te", "wp", 2 * len(inner))
            wc, ws = T.pc, T.ps
        h = T["h%d" % i]
        last = {"sc": 0, "ve": 0}
        for b in range(4):
            k = 4 * i + b
            bank = k % RING
            if k >= RING:
                wait("te", freed[k - RING][0], freed[k - RING][1])
            z = T.acc[:, BANK * bank:BANK * bank + n]
            m = done("te", g.tensor.matmul_mx(z, wc[:, 128 * b:128 * b + 128], ws[:, 128 * b:128 * b + 128],
                                              xc[:, ca:cb], xs[:, ca:cb], True, True))
            out = h[:, b:4 * n:4]
            if b % 2 == 0:
                wait("sc", "te", m)
                last["sc"] = done("sc", g.scalar.activation(out, z, ActivationFunctionType.Relu, scale=SCALE))
                freed[k] = ("sc", last["sc"])
            else:
                wait("ve", "te", m)
                last["ve"] = done("ve", g.vector.tensor_scalar(out, z, 0.0, SCALE, AluOpType.max, AluOpType.mult))
                freed[k] = ("ve", last["ve"])
        wait("ve", "sc", last["sc"])
        wait("ve", "ve", last["ve"])
        made[i] = done("ve", g.vector.quantize_mx(T["hc%d" % i][:, 0:n], T["hs%d" % i][:, 0:n], h[:, 0:4 * n]))

    def second(i):
        tile, w, ca, cb = units[i]
        n = cb - ca
        wc, ws = (T.wc, T.ws) if w == 0 else (T.pc, T.ps)
        bank = OWN_BANK if tile is None else FAR_BANK
        if tile is not None and w == 0 and copied[0]:
            wait("te", "sc", copied[0])
        wait("te", "ve", max(made[i], qw2))
        yp = T.acc[:, BANK * bank:BANK * bank + n]
        m = done("te", g.tensor.matmul_mx(yp, wc[:, W1C:WC], ws[:, W1C:WC],
                                          T["hc%d" % i][:, 0:n], T["hs%d" % i][:, 0:n], w == 0, w == 1))
        if tile is None:
            own_done[0] = m
        elif w == 1:
            yo = T["yo%d" % tile]
            wait("sc", "te", m)
            copied[0] = done("sc", g.scalar.activation(yo[:, ca:cb], yp, ActivationFunctionType.Copy))
            wait("g", "sc", copied[0])
            for dst, c, a, b in y_legs(core, tile):
                if a == ca:
                    buf, sem = y_slot(core, c, a) if dst == c else ("ry%d" % tile, "ry%d" % tile)
                    send([(dst, es, sem, T[buf][:, a:b], yo[:, a:b])])

    early, late = back[core]
    n0 = len(es) * len(y_legs(early, todo[early].index(core)))
    n1 = len(y_legs(late, todo[late].index(core)))
    own_last = not any(topo.may_write(c, core) for c in todo[core])
    added = 0

    pending = None
    for i in range(len(units)):
        if pending is not None and (units[i][0] is None) != (units[pending][0] is None):
            second(pending)
            pending = None
            if own_last and i == len(units) - 1:
                wait("ve", "y0", n0)
                for k in range(n1):
                    wait("ve", ("y1a", "y1b")[k], len(es))
                added = done("ve", g.vector.tensor_tensor(T.yt[:], T.yl0[:], T.yl1[:], AluOpType.add))
        first(i)
        if pending is not None:
            second(pending)
        pending = i
    second(pending)

    wait("ve", "te", own_done[0])
    base = BANK * OWN_BANK
    if not own_last:
        wait("ve", "y0", n0)
        added = done("ve", g.vector.tensor_tensor(T.yt[:], T.acc[:, base:base + NC], T.yl0[:], AluOpType.add))
    wait("ve", "ve", added)
    for k, q in ((0, "sy"), (1, "sc")):
        a, b = k * HC, (k + 1) * HC
        if k < n1:
            wait("ve", ("y1a", "y1b")[k], len(es))
        rest = T.acc[:, base + a:base + b] if own_last else T.yl1[:, a:b]
        t = done("ve", g.vector.tensor_tensor(T.yf[:, a:b], rest, T.yt[:, a:b], AluOpType.add))
        wait(q, "ve", t)
        Q[q].dma_start(T.y[:, a:b], T.yf[:, a:b]).then_inc(S["st%d" % k], 16)
    wait("sy", "st0", 16)
    wait("sc", "st1", 16)
    wait("g", "te", cnt["te"])
    wait("g", "sc", cnt["sc"])
    wait("g", "ls", sent[0])
    wait("g", "ve", cnt["ve"])
